import numpy as np, ml_dtypes
CORES = [5,29,101,125,133,157,229,253]
N = 8
BF = ml_dtypes.bfloat16
W, TU, RO, Q, S = 4096, 256, 4, 9, 16
HOPS = [4, 1]
BL = TU // len(HOPS)
def pack(x, l, w, k, h):
    return {"field": x.reshape(N, 128, W).astype(np.float32).astype(BF), "tube": np.ascontiguousarray(l.reshape(N, 128, TU)).astype(np.int32),
            "wt": w.reshape(N, 128, 1).astype(np.int32), "kn": k.reshape(N, 128, 1).astype(np.int32), "lim": np.ascontiguousarray(h.reshape(N, 128, RO)).astype(np.int32)}
def parts(rng):
    dark = rng.random((N, 8, 1, W)) < rng.choice(np.array([0.04, 0.08, 0.15]), (N, 8, 1, 1))
    x = np.where(dark, rng.integers(0, 64, (N, 8, 16, W), dtype=np.int16), rng.integers(48, 256, (N, 8, 16, W), dtype=np.int16))
    l = rng.integers(0, W, (N, 8, 16, TU)); w = rng.integers(0, 256, (N, 8, 16)); k = rng.integers(0, 256, (N, 8, 16))
    return x, l, w, k, rng.integers(16, 72, (N, 8, 16, RO))
def setup_inputs(rng):
    return pack(*parts(rng))
def setup_inputs_spread(rng):
    sh = rng.choice(np.array([0, 0, 0, 0, 0, 1, 1, 2, 4, 8], np.int16), (N, 8, 1, W))
    x = rng.integers(0, 256, (N, 8, 16, W), dtype=np.int16) >> sh
    l = rng.integers(0, W, (N, 8, 16, TU)); l[:, 1::2] = np.minimum((W * rng.random((N, 4, 16, TU)) ** 3).astype(np.int64), W - 1)
    w = rng.integers(0, 256, (N, 8, 16)) >> rng.integers(0, 9, (N, 8, 16)); k = rng.integers(0, 256, (N, 8, 16)) >> rng.integers(0, 9, (N, 8, 16))
    h = rng.integers(0, 249, (N, 8, 16, RO)) >> rng.integers(0, 9, (N, 8, 1, RO))
    return pack(x, l, w, k, h)
def ends_of(rng, hi, shape):
    return np.where(rng.random(shape) < 0.14, rng.integers(0, hi + 1, shape), hi * rng.integers(0, 2, shape))
def setup_inputs_ends(rng):
    kind = rng.random((N, 8, 1, W)); top = np.int16(255)
    x = np.where(kind < 0.7, top, np.where(kind < 0.82, np.int16(0), top * rng.integers(0, 2, (N, 8, 16, W), dtype=np.int16)))
    i = np.arange(16)[:, None]
    b = ((np.arange(N)[:, None] + np.arange(8)[None, :]) & 1) * (W - 1)
    l = np.where(i < rng.integers(0, 17, (N, 8, 1, TU)), b[:, :, None, None], (W - 1) * rng.integers(0, 2, (N, 8, 16, TU)))
    free = ((np.arange(TU) * 5) & 15) < 5; l[..., free] = rng.integers(0, W, (N, 8, 16, int(np.count_nonzero(free))))
    w = ends_of(rng, 255, (N, 8, 16)); k = ends_of(rng, 255, (N, 8, 16))
    h = 248 * rng.integers(0, 2, (N, 8, 16, RO)); h[:, 1::2] = 248 * rng.integers(0, 2, (N, 4, 1, RO))
    for q in range(N):
        for g in range(8):
            o = W - 1 - b[q, g]; x[q, g][:, b[q, g]] = 255
            x[q, g][:, o] = 0 if (g & 3) < 2 or q == 1 else 255 * rng.integers(0, 2, 16) if (g & 3) == 2 else 255
    h[0, :, :, 0] = 0; h[0, 0, :, 1] = 248; h[1, :, :, 0] = 248; h[1, 0, :, 1] = 0; l[1, :, 15, :] = (W - 1 - b[1])[:, None]
    h[2, :, :, 0] = 0; h[2, 0, :, 0] = 248; l[2, 0] = b[2, 0]; l[2, 0, 15, :7] = W - 1 - b[2, 0]; h[2, :, :, 1] = 248
    p = N - 1; u = (15 * 65025) & 4095
    for g in range(4, 8):
        x[p, g][:, 0] = 255; x[p, g][:, W - 1] = 255; w[p, g] = 255
        if g == 5: w[p, g] = 0; w[p, g, 0] = 16; w[p, g, 1] = 1; x[p, g, 1, 0] = 15; x[p, g, 1, W - 1] = 15
        if g > 5:
            w[p, g, 0] = 0; k[p, g] = 255 * (np.arange(16) & 1)
            for j in (0, W - 1):
                x[p, g][:, ((u * u >> 4) + j) & (W - 1)] = 0
                x[p, g][:, ((u * u >> 4) + 255 * u + j) & (W - 1)] = 255 if g == 6 else 0
    return pack(x, l, w, k, h)
def setup_inputs_corners(rng):
    x, l, w, k, h = parts(rng); i = np.arange(16)[:, None]; v = np.arange(TU)
    for q in range(N):
        for g in range(8):
            c = (g + q) & 7
            if c == 0: h[q, g] = 0
            if c == 1: h[q, g] = 248; x[q, g] = np.minimum(x[q, g], 247)
            if c == 2:
                s = rng.integers(0, W, TU); s[0] = 0; s[1] = W - 1; l[q, g] = s[None, :]
            if c == 3:
                m = np.where(rng.random(W) < 0.9, Q, Q - 1)[None, :]
                x[q, g] = np.where(i < m, rng.integers(150, 256, (16, W)), rng.integers(0, 90, (16, W))); h[q, g] = 100
            if c == 4: w[q, g] = 0; k[q, g] = 0
            if c == 5:
                m = rng.random(W) < 0.9; x[q, g, 0, m] = 255; x[q, g, 1, m] = 15; w[q, g] = 0; w[q, g, 0] = 16; w[q, g, 1] = 1; k[q, g] = 255 * rng.integers(0, 2, 16)
            if c == 6:
                t = rng.integers(0, 4, (16, TU)); l[q, g] = np.where(t == 0, 0, np.where(t == 1, W - 1, np.where(t == 2, S * v, S * v + S - 1)))
            if c == 7:
                x[q, g][:, 0::2] = rng.integers(200, 256, (16, W // 2)); x[q, g][:, 1::2] = rng.integers(0, 64, (16, W // 2)); h[q, g] = 100
                l[q, g] = 2 * rng.integers(0, W // 2, (16, TU)) + (i == (v % 17)[None, :])
    return pack(x, l, w, k, h)
def setup_inputs_ties(rng):
    x, l, w, k, h = parts(rng)
    pr = 60 + 4 * rng.integers(0, 3, (N, 8, 16, 5)); x = np.take_along_axis(pr, np.broadcast_to(rng.integers(0, 5, (N, 8, 1, W)), (N, 8, 16, W)), 3)
    return pack(x, l, w, k, rng.integers(53, 66, (N, 8, 16, RO)))
def setup_inputs_brink(rng):
    x, l, w, k, h = parts(rng); r0 = int(rng.integers(0, 8)); v = np.arange(TU)
    h[..., 0] = 0; h[..., 1] = 248; h[..., 2:] = rng.integers(246, 249, (N, 8, 1, RO - 2))
    for g in range(8):
        c = (g + r0) & 7; low = rng.permutation(W)[:32]
        for q in range(N):
            if c < 4:
                o = rng.permutation(16); y = np.full((16, W), 254); y[o[:Q]] = 255
                b = np.nonzero(rng.random(W) < 0.1)[0]; y[o[rng.integers(0, Q, len(b))], b] = 254
                x[q, g] = y
            elif c < 6:
                x[q, g] = rng.integers(248, 256, (16, W)); x[q, g][:, low] = rng.integers(7, 9, (16, 32))
            else:
                x[q, g] = rng.integers(243, 256, (16, W)); x[q, g][:, low] = rng.integers(0, 4, (16, 32))
            if c >= 4:
                l[q, g, rng.integers(1, 16, TU), v] = low[rng.integers(0, 32, TU)]; h[q, g] = 0
            if c == 0:
                d = int(rng.integers(0, W)); s = rng.integers(0, W - 1, (16, TU)); l[q, g] = s + (s >= d)
                l[q, g, rng.integers(1, 16, 7), rng.permutation(TU)[:7]] = d
                x[q, g][:, d] = rng.integers(0, 248, 16); h[q, g, :, 0] = 248
    return pack(x, l, w, k, h)
def check_inputs(d):
    bad = []
    for a, lo, hi in (("field", 0, 255), ("tube", 0, W - 1), ("wt", 0, 255), ("kn", 0, 255), ("lim", 0, 248)):
        v = np.asarray(d[a]).astype(np.float64)
        if not (np.min(v) >= lo and np.max(v) <= hi): bad.append("range of " + a)
        elif np.any(v != np.floor(v)): bad.append("whole numbers of " + a)
    return bad
def reference(field, tube, wt, kn, lim):
    x = field.astype(np.float32).astype(np.int32).reshape(N, 8, 16, W)
    l = tube.astype(np.int64).reshape(N, 8, 16, TU)
    w = wt.astype(np.int64).reshape(N, 8, 16, 1); k = kn.astype(np.int64).reshape(N, 8, 16, 1); h = lim.astype(np.int64).reshape(N, 8, 16, RO)
    cut = [0] * N; v = np.arange(TU); j = np.arange(16)[:, None]
    for rnd in range(RO):
        if rnd: l = np.concatenate([np.roll(l[..., b * BL:(b + 1) * BL], HOPS[b], axis=0) for b in range(len(HOPS))], axis=-1)
        nl = np.zeros((N, 8, 16, TU), np.int64); nz = np.zeros((N, 8, 16, TU), np.int64); ncut = [0] * N
        for q in range(N):
            for g in range(8):
                X, L = x[q, g], l[q, g]
                M = np.minimum.accumulate(X[:, L], axis=1)
                holds = (M >= (h[q, g, :, rnd] + (cut[q] & 7))[:, None, None]).astype(np.int64)
                ok = (np.add.reduce(holds, axis=0) >= Q).astype(np.int64)
                m = np.maximum(np.add.reduce(ok, axis=0), 1) - 1
                Z = np.take_along_axis(M, np.broadcast_to(m[None, None, :], (16, 1, TU)), 1)[:, 0].astype(np.int64)
                u = np.add.reduce(w[q, g] * X[:, L[m, v]], axis=0) & 4095
                c = ((u * u >> 4)[None, :] + k[q, g] * u[None, :] + L) & (W - 1)
                s = np.add.reduce(np.abs(X[:, c] - Z[:, None, :]), axis=0)
                best = c[np.argmin(s, axis=0), v]
                back = L[np.clip(m[None, :] + 1 - j, 0, 15), v[None, :]]
                nl[q, g] = np.where(j == 0, best[None, :], np.where(j <= m[None, :], back, c)); nz[q, g] = Z
                y = (Z + X[:, best]) >> 1
                x[q, g][:, S * v + (u & (S - 1))] = y
                ncut[q] += int(np.count_nonzero(m < 15))
        l = nl; cut = ncut
    return {"yl": l.reshape(N, 128, TU).astype(np.float32), "yz": nz.reshape(N, 128, TU).astype(np.float32)}

@@ -1,0 +1,520 @@
+from concourse.mybir import dt, AluOpType, ActivationFunctionType
+
+N, RO, TU, BL = 8, 4, 256, 128
+HOPS = [4, 1]
+NE = 8
+A_ = AluOpType
+F_ = ActivationFunctionType
+BIG = 1.5 * 2.0 ** 35
+
+SCRATCH = {}
+
+
+def buf(name, cols, dtype, where="sbuf"):
+    SCRATCH[name] = (where, [128, cols], dtype)
+
+
+for _n in ("xs", "gg", "mm", "hb", "hh", "aa"):
+    buf(_n, 4096, "bfloat16")
+buf("l0", 256, "int32"); buf("lo0", 256, "uint16")
+buf("rel", BL * 3, "uint16"); buf("land", BL * 6, "uint16"); buf("nb", BL * 6, "uint16")
+PART = {}
+for _t in range(1, RO):
+    PART["rel%d" % _t] = ("rel", BL * (_t - 1))
+    for _b in (0, 1):
+        PART["land%d%d" % (_t, _b)] = ("land", BL * (2 * _t - 2 + _b))
+        PART["nb%d%d" % (_t, _b)] = ("nb", BL * (2 * _t - 2 + _b))
+
+
+def at(name, a=0, b=BL):
+    n, o = PART[name]
+    return n, o + a, o + b
+
+
+for _b in (0, 1):
+    for _n, _c, _d in (("lf", 128, "float32"), ("lp", 64, "float32"), ("lq", 128, "float32"), ("sk", 1024, "float32"),
+                       ("ok", 128, "bfloat16"), ("ms", 136, "bfloat16"), ("ofm", 16, "uint16"), ("zt", 128, "bfloat16"),
+                       ("rr", 128, "float32"), ("ww", 128, "float32"), ("ci", 128, "int32"), ("cc", 128, "int32"),
+                       ("ofc", 128, "uint16"), ("ks", 128, "float32"), ("kr", 128, "float32"), ("oh", 128, "bfloat16"),
+                       ("ot", 128, "bfloat16"), ("pb", 128, "float32"), ("mt", 128, "bfloat16"), ("ofi", 8, "uint16"),
+                       ("rp", 128, "int32"), ("rv", 128, "int32"), ("rest", 128, "float32"), ("out", 128, "float32"),
+                       ("zo", 128, "float32")):
+        buf(_n + str(_b), _c, _d)
+for _n, _c, _d in (("xl", 256, "bfloat16"), ("zz", 256, "bfloat16"), ("yi", 256, "int32"), ("y2", 256, "int32"),
+                   ("ofs", 16, "uint16"), ("uw", 16, "int32"), ("u15", 16, "int32"), ("uv", 16, "int32"),
+                   ("ei", 1, "int32"), ("ea", 1, "int32"), ("thr", 4, "float32"), ("nth", 4, "float32"),
+                   ("bm", 128, "float32"), ("km", 128, "float32"), ("kq", 8, "float32"), ("kd", 8, "int32"),
+                   ("csf", 16, "float32"), ("cvf", 16, "float32"),
+                   ("wi", 1, "int32"), ("ki", 1, "int32"), ("li", 4, "int32"),
+                   ("pc", 1, "int32"), ("pi", 1, "int32"), ("pg", 1, "int32"), ("row", 128, "int32"), ("r15", 128, "int32"),
+                   ("r16", 128, "int32"), ("cols", 24, "float32"), ("tq", 128, "float32"),
+                   ("bo", 128, "bfloat16"), ("qp", 128, "bfloat16"),
+                   ("mk", 136, "bfloat16"), ("idb", 128, "bfloat16"), ("nid", 128, "bfloat16"), ("idf", 128, "float32"),
+                   ("r0f", 128, "float32"), ("bom", 136, "bfloat16"), ("boi", 128, "bfloat16"), ("wb", 128, "bfloat16"),
+                   ("ind", 2048, "bfloat16"), ("wr", 2048, "bfloat16"), ("sh", 1920, "float32"), ("ex", 2048, "bfloat16"),
+                   ("ones", 2048, "bfloat16"), ("rst", 1024, "bfloat16"), ("rs2", 128, "float32"), ("kc", 128, "bfloat16"),
+                   ("irow", 128, "bfloat16"), ("cr", 16, "float32"), ("cw", 16, "float32"), ("cv", 16, "bfloat16"),
+                   ("cvs", 16, "int32"), ("cs", 16, "bfloat16"), ("g8", 8, "bfloat16"), ("koi", 8, "int32"), ("kof", 8, "uint16")):
+    buf(_n, _c, _d)
+for _n in range(8):
+    buf("q%d" % _n, 512, "float32", "psum")
+
+SEMAPHORES = ["sV", "sS", "sT", "sG", "dx", "dt", "dw", "dk", "dl", "lsem", "o00", "o01", "o10", "o11"]
+SEMAPHORES += ["a%d%d" % (_t, _b) for _t in range(1, RO) for _b in (0, 1)] + ["h%d" % _t for _t in range(1, RO)]
+
+BIG16 = 1.5 * 2.0 ** 27
+TAIL = 0
+CH = 64
+
+CYC, TEC = 0.00083, 0.000417
+
+
+def build():
+    ops = []
+
+    def add(q, cost, fn, rd, wr, n=1, late=0.0, gat=False):
+        ops.append(dict(q=q, c=cost, fn=fn, rd=rd, wr=wr, n=n, late=late, gat=gat))
+
+    def whole(*names):
+        return [(x, 0, SCRATCH[x][1][1]) for x in names]
+
+    def R(x):
+        return [y if isinstance(y, tuple) else at(y) if y in PART else whole(y)[0] for y in x]
+
+    def V(cyc, fn, rd, wr):
+        add("V", max(64, cyc) * CYC + 0.02, lambda e, T: [fn(e, T)], R(rd), R(wr))
+
+    def S(cyc, fn, rd, wr):
+        add("S", cyc * CYC + 0.065, lambda e, T: [fn(e, T)], R(rd), R(wr))
+
+    def TE(cyc, fn, rd, wr, n=1):
+        add("T", cyc * TEC + 0.03, fn, R(rd), R(wr), n)
+
+    def GP(cyc, fn, rd, wr):
+        add("G", 0.17 + cyc * CYC, lambda e, T: [fn(e, T)], R(rd), R(wr))
+
+    def ev(sem, val, buf, late):
+        add("E", 0.0, (sem, val), [], R([buf]), 0, late)
+
+    def ts(out, in0, s1, s2, *op):
+        return lambda e, T: e.tensor_scalar(out(T), in0(T), s1(T) if callable_(s1) else s1, s2(T) if callable_(s2) else s2, *op)
+
+    def callable_(x):
+        return not isinstance(x, (int, float)) and x is not None
+
+    def tt(out, a, b, op):
+        return lambda e, T: e.tensor_tensor(out(T), a(T), b(T), op)
+
+    def tc(out, a):
+        return lambda e, T: e.tensor_copy(out(T), a(T))
+
+    def P(name, a=None, b=None):
+        if name in PART:
+            name, a, b = at(name) if a is None else at(name, a, b)
+        return (lambda T: T[name][:, :]) if a is None else (lambda T: T[name][:, a:b])
+
+    def col(j):
+        return P("cols", j, j + 1)
+
+    ev("dx", 16, "xs", 6.0); ev("dt", 16, "l0", 3.0); ev("dw", 16, "wi", 2.5); ev("dk", 16, "ki", 2.5); ev("dl", 16, "li", 2.5)
+    GP(2, lambda e, T: e.iota(T.pc[:, :], [[0, 1]], 0, 1), [], ["pc"])
+    GP(256, lambda e, T: e.iota(T.row[:, :], [[1, 128]], 0, 0), [], ["row"])
+    GP(16, lambda e, T: e.iota(T.koi[:, :], [[16, 8]], 15, 0), [], ["koi"])
+    GP(32, lambda e, T: e.iota(T.cr[:, :], [[1, 16]], 0, 0, allow_small_or_imprecise_dtypes=True), [], ["cr"])
+    GP(32, lambda e, T: e.iota(T.cw[:, :], [[0, 4], [16, 4]], 0, 0, allow_small_or_imprecise_dtypes=True), [], ["cw"])
+    V(1024, lambda e, T: e.memset(T.ones[:, :], 1.0), [], ["ones"])
+    GP(4096, lambda e, T: e.affine_select(T.ex[:, :], T.ones[:, :], [[-1, 128], [0, 16]], A_.is_equal, 0.0, 0, 1), ["ones"], ["ex"])
+    V(512, lambda e, T: e.memset(T.rst[:, :], 0.0), [], ["rst"])
+    V(64, lambda e, T: e.memset(T.rst[:, 0::16], 1024.0), [], ["rst"])
+    V(128, lambda e, T: e.memset(T.rs2[:, :], 0.0), [], ["rs2"])
+    V(64, lambda e, T: e.memset(T.rs2[:, 0::16], 1048576.0), [], ["rs2"])
+    V(64, lambda e, T: e.memset(T.kc[:, :], 0.5), [], ["kc"])
+    V(64, lambda e, T: e.memset(T.kc[0:1, :], -2048.0), [], ["kc"])
+    for b in (0, 1):
+        V(64, lambda e, T, b=b: e.memset(T["sk%d" % b][:, 0:64], 0.0), [], [("sk%d" % b, 0, 64)])
+    V(1, ts(P("pi"), P("pc"), 15, None, A_.bitwise_and), ["pc"], ["pi"])
+    V(1, ts(P("pg"), P("pc"), 112, None, A_.bitwise_and), ["pc"], ["pg"])
+    V(1, tc(col(0), P("pi")), ["pi"], [("cols", 0, 1)])
+    V(1, tc(col(1), P("pg")), ["pg"], [("cols", 1, 2)])
+    V(1, ts(col(2), P("pi"), 1.0, None, A_.is_ge), ["pi"], [("cols", 2, 3)])
+    V(1, ts(col(3), P("pi"), 15.0, None, A_.is_ge), ["pi"], [("cols", 3, 4)])
+    V(1, ts(col(4), col(2), 20.75, -20.0, A_.mult, A_.add), [("cols", 2, 3)], [("cols", 4, 5)])
+    V(1, ts(col(5), P("pi"), 16.0, None, A_.mult), ["pi"], [("cols", 5, 6)])
+    V(1, ts(col(6), P("pg"), 0.0625, None, A_.mult), ["pg"], [("cols", 6, 7)])
+    V(1, tc(col(7), P("wi")), ["wi"], [("cols", 7, 8)])
+    V(1, ts(col(8), P("ki"), 8.0, 2047.5, A_.mult, A_.add), ["ki"], [("cols", 8, 9)])
+    V(1, tc(col(10), P("ki")), ["ki"], [("cols", 10, 11)])
+    V(1, ts(col(9), P("ki"), col(10), -64.0, A_.mult, A_.mult), ["ki", ("cols", 10, 11)], [("cols", 9, 10)])
+    V(1, tc(P("thr", 0, 1), P("li", 0, 1)), ["li"], [("thr", 0, 1)])
+    V(1, ts(P("nth", 0, 1), P("li", 0, 1), -1.0, 0.5, A_.mult, A_.add), ["li"], [("nth", 0, 1)])
+    V(128, ts(P("r15"), P("row"), 15, None, A_.bitwise_and), ["row"], ["r15"])
+    V(128, ts(P("r16"), P("row"), 112, None, A_.bitwise_and), ["row"], ["r16"])
+    c = lambda j: ("cols", j, j + 1)
+    V(128, ts(P("bo"), P("r16"), col(1), None, A_.is_equal), ["r16", c(1)], ["bo"])
+    V(128, ts(P("tq"), P("r15"), 1.0, None, A_.add), ["r15"], ["tq"])
+    V(256, tt(P("qp"), P("tq"), P("bo"), A_.mult), ["tq", "bo"], ["qp"])
+    for i in range(16):
+        V(64, ts(P("ind", 128 * i, 128 * i + 128), P("qp"), float(i + 1), None, A_.is_equal), ["qp"], [("ind", 128 * i, 128 * i + 128)])
+    V(128, ts(P("mk", 0, 128), P("r15"), col(0), None, A_.is_equal), ["r15", c(0)], [("mk", 0, 128)])
+    V(1, lambda e, T: e.memset(T.mk[:, 128:136], 1.0), [], [("mk", 128, 136)])
+    V(128, ts(P("bom", 0, 128), P("bo"), col(2), None, A_.mult), ["bo", c(2)], [("bom", 0, 128)])
+    V(1, tc(P("bom", 128, 129), col(3)), [c(3)], [("bom", 128, 129)])
+    V(64, ts(P("boi"), P("bo"), col(0), None, A_.mult), ["bo", c(0)], ["boi"])
+    V(64, ts(P("wb"), P("bo"), col(7), None, A_.mult), ["bo", c(7)], ["wb"])
+    V(256, tt(P("idb"), P("bo"), P("mk", 0, 128), A_.mult), ["bo", ("mk", 0, 128)], ["idb"])
+    S(128, lambda e, T: e.activation(T.nid[:, :], T.idb[:, :], F_.Copy, scale=-1.0), ["idb"], ["nid"])
+    S(128, lambda e, T: e.activation(T.idf[:, :], T.idb[:, :], F_.Copy), ["idb"], ["idf"])
+    V(128, ts(P("r0f"), P("qp"), 1.0, None, A_.is_equal), ["qp"], ["r0f"])
+    V(128, tc(P("irow"), P("r15")), ["r15"], ["irow"])
+    V(64, ts(P("cs", 0, 8), P("cr", 0, 8), col(6), None, A_.is_equal), ["cr", c(6)], [("cs", 0, 8)])
+    V(64, ts(P("cs", 8, 16), P("cr", 0, 8), col(6), 64.0, A_.is_equal, A_.mult), ["cr", c(6)], [("cs", 8, 16)])
+    V(64, ts(P("g8"), P("cr", 0, 8), col(6), 16.0, A_.is_equal, A_.mult), ["cr", c(6)], ["g8"])
+    V(64, ts(P("cv", 0, 8), P("cr", 0, 8), 256.0, col(5), A_.mult, A_.add), ["cr", c(5)], [("cv", 0, 8)])
+    V(64, ts(P("cv", 8, 16), P("cw", 0, 8), col(0), None, A_.add), ["cw", c(0)], [("cv", 8, 16)])
+    V(64, ts(P("cvs"), P("cr"), 256.0, col(5), A_.mult, A_.add), ["cr", c(5)], ["cvs"])
+    V(64, tc(P("kof"), P("koi")), ["koi"], ["kof"])
+    V(128, ts(P("bm"), P("qp"), 2.0, col(2), A_.is_ge, A_.mult), ["qp", c(2)], ["bm"])
+    for y in range(1, 16):
+        GP(256, lambda e, T, y=y: e.affine_select(T.sh[:, 128 * (y - 1):128 * y], T.bm[:, :], [[-16, 8], [1, 16]], A_.is_equal, 0.0, -(y + 1), 1), ["bm"], [("sh", 128 * (y - 1), 128 * y)])
+    S(2048, lambda e, T: e.activation(T.wr[:, :], T.ind[:, :], F_.Copy, scale=T.cols[:, 7:8]), ["ind", c(7)], ["wr"])
+    V(64, ts(P("csf", 0, 8), P("cr", 0, 8), col(6), None, A_.is_equal), ["cr", c(6)], [("csf", 0, 8)])
+    V(64, ts(P("csf", 8, 16), P("cr", 0, 8), col(6), None, A_.is_equal), ["cr", c(6)], [("csf", 8, 16)])
+    V(64, lambda e, T: e.memset(T.cvf[:, 0:8], -7.5), [], [("cvf", 0, 8)])
+    V(64, ts(P("cvf", 8, 16), P("cr", 0, 8), 256.0, col(5), A_.mult, A_.add), ["cr", c(5)], [("cvf", 8, 16)])
+
+    def mm(e, out, l, r, st, sp):
+        return e.matmul(out, l, r, st, sp)
+
+    for t in range(RO):
+        first = len(ops)
+        for b in (1 - TAIL, TAIL):
+            tag(ops, first, 1 - b)
+            first = len(ops)
+            sb = str(b)
+            QA, QB, QC, QD = "q%d" % (2 * b), "q%d" % (2 * b + 1), "q%d" % (4 + 2 * b), "q%d" % (5 + 2 * b)
+            o = 2048 * b
+            if t == 0:
+                off = lambda v0, v1, b=b: P("lo0", 128 * b + v0, 128 * b + v1)
+                V(128, tc(P("lo0", 128 * b, 128 * b + 128), P("l0", 128 * b, 128 * b + 128)), [("l0", 128 * b, 128 * b + 128)], [("lo0", 128 * b, 128 * b + 128)])
+                ob = ("lo0", 128 * b, 128 * b + 128)
+                V(128, tc(P("lf" + sb), P("l0", 128 * b, 128 * b + 128)), [("l0", 128 * b, 128 * b + 128)], ["lf" + sb])
+            else:
+                ln = "land%d%d" % (t, b)
+                ops.append(dict(q="E", c=0.0, fn=("a%d%d" % (t, b), NE), rd=[], wr=R([ln]), n=0, late=4.5 if b else 2.8, after=(t - 1, b)))
+                off = lambda v0, v1, ln=ln: P(ln, v0, v1)
+                ob = at(ln)
+                V(128, tc(P("lf" + sb), P(ln)), [ln], ["lf" + sb])
+
+            for v0 in range(0, 128, CH):
+                c0, c1 = o + 16 * v0, o + 16 * (v0 + CH)
+                gat(add, "gg", c0, c1, off(v0, v0 + CH), ob)
+                V((c1 - c0) // 2, lambda e, T, c0=c0, c1=c1: e.tensor_tensor_scan(T.mm[:, c0:c1], T.rst[:, 0:c1 - c0], T.gg[:, c0:c1], 0.0, A_.add, A_.min),
+                  ["rst", ("gg", c0, c1)], [("mm", c0, c1)])
+                held(add, c0, c1, t)
+                TE(16 * 64, lambda e, T, v0=v0, c0=c0, c1=c1, QA=QA, CH=CH: [e.matmul(T[QA][:, v0:v0 + CH], T.ind[:, 128 * i:128 * i + 128], T.hb[:, c0 + i:c1:16], i == 0, i == 15) for i in range(16)],
+                   ["ind", ("hb", c0, c1)], [(QA, v0, v0 + CH)], 16)
+            S(128, lambda e, T, sb=sb: e.activation(T["lq" + sb][:, :], T["lf" + sb][:, :], F_.Identity, bias=T.cols[:, 9:10], scale=16.0), ["lf" + sb, c(9)], ["lq" + sb])
+            S(64, lambda e, T, sb=sb, QD=QD: e.activation(T[QD][:, 0:64], T["lf" + sb][:, 0:64], F_.Copy, scale=4096.0), ["lf" + sb], [(QD, 0, 64)])
+            V(64, tt(P("lp" + sb), P("lf" + sb, 64, 128), P(QD, 0, 64), A_.add), ["lf" + sb, (QD, 0, 64)], ["lp" + sb])
+            for Q, y0, y1 in ((QC, 1, 8), (QD, 8, 16)):
+                n = y1 - y0
+                TE(n * 256, lambda e, T, Q=Q, y0=y0, y1=y1, sb=sb: [e.matmul(T[Q][:, 64 * (y - y0):64 * (y - y0) + 64], T.sh[:, 128 * (y - 1):128 * y], T["lp" + sb][:, :], True, True) for y in range(y0, y1)],
+                   ["sh", "lp" + sb], [(Q, 0, 64 * n)], n)
+                S(64 * n, lambda e, T, Q=Q, n=n, y0=y0, sb=sb: e.activation(T["sk" + sb][:, 64 * y0:64 * y0 + 64 * n], T[Q][:, 0:64 * n], F_.Copy), [(Q, 0, 64 * n)], [("sk" + sb, 64 * y0, 64 * y0 + 64 * n)])
+            V(128, ts(P("ok" + sb), P(QA, 0, 128), col(4), None, A_.is_ge), [(QA, 0, 128), c(4)], ["ok" + sb])
+            TE(129, lambda e, T, sb=sb, QA=QA: [e.matmul(T[QA][:, 128:257], T["ok" + sb][:, :], T.bom[:, 0:129], True, True)], ["ok" + sb, ("bom", 0, 129)], [(QA, 128, 257)])
+            V(129, tt(P("ms" + sb, 0, 129), P("mk", 0, 129), P(QA, 128, 257), A_.mult), ["mk", (QA, 128, 257)], [("ms" + sb, 0, 129)])
+            TE(128, lambda e, T, sb=sb, QA=QA: [e.matmul(T[QA][:, 264:280], T["ms" + sb][:, 0:128], T.cs[:, :], True, False), e.matmul(T[QA][:, 264:280], T.idb[:, :], T.cv[:, :], False, True)],
+               [("ms" + sb, 0, 129), "cs", "idb", "cv"], [(QA, 264, 280)], 2)
+            V(64, tc(P("ofm" + sb), P(QA, 264, 280)), [(QA, 264, 280)], ["ofm" + sb])
+            gat(add, "xl", 128 * b, 128 * b + 128, P("ofm" + sb, 0, 8), ("ofm" + sb, 0, 16), ("gg", o, o + 2048))
+            gat(add, "zz", 128 * b, 128 * b + 128, P("ofm" + sb, 0, 8), ("ofm" + sb, 0, 16), ("mm", o, o + 2048))
+            TE(192, lambda e, T, b=b, QB=QB: [e.matmul(T[QB][:, 0:128], T.wb[:, :], T.xl[:, 128 * b:128 * b + 128], True, False), e.matmul(T[QB][:, 0:128], T.kc[0:2, :], T.ones[0:2, 0:128], False, True)],
+               ["wb", ("xl", 128 * b, 128 * b + 128), "kc", "ones"], [(QB, 0, 128)], 2)
+            V(128, ts(P("rr" + sb), P(QB, 0, 128), BIG, BIG, A_.add, A_.subtract), [(QB, 0, 128)], ["rr" + sb])
+            V(128, tt(P("ww" + sb), P(QB, 0, 128), P("rr" + sb), A_.subtract), [(QB, 0, 128), "rr" + sb], ["ww" + sb])
+            S(128, lambda e, T, sb=sb, QB=QB: e.activation(T[QB][:, 128:256], T["ww" + sb][:, :], F_.Square, bias=T.cols[:, 8:9]), ["ww" + sb, c(8)], [(QB, 128, 256)])
+            V(128, tt(P("ci" + sb), P("lq" + sb), P(QB, 128, 256), A_.add), ["lq" + sb, (QB, 128, 256)], ["ci" + sb])
+            V(128, ts(P("cc" + sb), P("ci" + sb), 4, 4095, A_.arith_shift_right, A_.bitwise_and), ["ci" + sb], ["cc" + sb])
+            V(128, tc(P("ofc" + sb), P("cc" + sb)), ["cc" + sb], ["ofc" + sb])
+            TE(128, lambda e, T, b=b, QD=QD: [e.matmul(T[QD][:, 0:128], T.zz[:, 128 * b:128 * b + 128], T.nid[:, :], True, True)], [("zz", 128 * b, 128 * b + 128), "nid"], [(QD, 0, 128)])
+            S(128, lambda e, T, sb=sb, QD=QD: e.activation(T["zt" + sb][:, :], T[QD][:, 0:128], F_.Copy), [(QD, 0, 128)], ["zt" + sb])
+            for k in range(4):
+                Q = (QC, QD)[k % 2]
+                c0, c1 = o + 512 * k, o + 512 * k + 512
+                gat(add, "hh", c0, c1, P("ofc" + sb, 32 * k, 32 * k + 32), ("ofc" + sb, 0, 128))
+                TE(1024, lambda e, T, Q=Q, c0=c0, c1=c1, k=k, sb=sb: [e.matmul(T[Q][:, :], T["zt" + sb][:, :], T.ex[:, 512 * k:512 * k + 512], True, False), e.matmul(T[Q][:, :], T.idb[:, :], T.hh[:, c0:c1], False, True)],
+                   ["zt" + sb, "ex", "idb", ("hh", c0, c1)], [Q], 2)
+                S(512, lambda e, T, Q=Q, c0=c0, c1=c1: e.activation(T.aa[:, c0:c1], T[Q][:, :], F_.Abs), [Q], [("aa", c0, c1)])
+            V(270, lambda e, T, sb=sb: e.tensor_copy(T["rp" + sb][:, :], T["sk" + sb][:, :].indirect(T["ofm" + sb][:, 8:16])), ["sk" + sb, ("ofm" + sb, 0, 16)], ["rp" + sb])
+            V(64, ts(P("rv" + sb, 0, 64), P("rp" + sb, 0, 64), 12, None, A_.arith_shift_right), ["rp" + sb], [("rv" + sb, 0, 64)])
+            V(64, ts(P("rv" + sb, 64, 128), P("rp" + sb, 64, 128), 4095, None, A_.bitwise_and), ["rp" + sb], [("rv" + sb, 64, 128)])
+            TE(256, lambda e, T, sb=sb, QA=QA: [e.matmul(T[QA][:, 280:408], T.nid[:, :], T["ok" + sb][:, :], True, False), e.matmul(T[QA][:, 280:408], T.ones[0:1, 0:128], T.ones[0:1, 0:128], False, True)],
+               ["nid", "ok" + sb, "ones"], [(QA, 280, 408)], 2)
+            V(128, tt(P(QA, 0, 128), P("cc" + sb), P(QA, 280, 408), A_.mult), ["cc" + sb, (QA, 280, 408)], [(QA, 0, 128)])
+            V(128, tt(P("rest" + sb), P("rv" + sb), P(QA, 0, 128), A_.add), ["rv" + sb, (QA, 0, 128)], ["rest" + sb])
+            TE(16 * 64 + 128, lambda e, T, o=o, QB=QB: [e.matmul(T[QB][:, 384:512], T.ones[0:1, 0:128], T.irow[0:1, :], True, False)] +
+               [e.matmul(T[QB][:, 384 + i:512:16], T.aa[:, o + i:o + 2048:16], T.g8[:, :], False, i == 15) for i in range(16)],
+               ["ones", "irow", ("aa", o, o + 2048), "g8"], [(QB, 384, 512)], 17)
+            V(128, lambda e, T, sb=sb, QB=QB: e.tensor_tensor_scan(T["ks" + sb][:, :], T.rs2[:, :], T[QB][:, 384:512], 0.0, A_.add, A_.min), ["rs2", (QB, 384, 512)], ["ks" + sb])
+            V(270, lambda e, T, sb=sb: e.tensor_copy(T["kr" + sb][:, :], T["ks" + sb][:, :].indirect(T.kof[:, :])), ["ks" + sb, "kof"], ["kr" + sb])
+            V(128, tt(P("oh" + sb), P("kr" + sb), P(QB, 384, 512), A_.is_equal), ["kr" + sb, (QB, 384, 512)], ["oh" + sb])
+            TE(128, lambda e, T, sb=sb, QA=QA: [e.matmul(T[QA][:, 0:128], T["oh" + sb][:, :], T.idb[:, :], True, True)], ["oh" + sb, "idb"], [(QA, 0, 128)])
+            V(128, tt(P("pb" + sb), P("cc" + sb), P(QA, 0, 128), A_.mult), ["cc" + sb, (QA, 0, 128)], ["pb" + sb])
+            TE(512, lambda e, T, sb=sb, QD=QD: [e.matmul(T[QD][:, 0:128], T.idf[:, :], T["rest" + sb][:, :], True, False)], ["idf", "rest" + sb], [(QD, 0, 128)])
+            TE(512, lambda e, T, sb=sb, QD=QD: [e.matmul(T[QD][:, 0:128], T.r0f[:, :], T["pb" + sb][:, :], False, True)], ["r0f", "pb" + sb], [(QD, 0, 128)])
+            if t < RO - 1:
+                nb = "nb%d%d" % (t + 1, b)
+                V(128, tc(P(nb), P(QD, 0, 128)), [(QD, 0, 128)], [nb])
+                ops.append(dict(q="G", c=1.0, fn=None, rd=R([nb]), wr=[], n=0, late=0.0, send=(t, b, nb)))
+                if b == TAIL:
+                    V(256, tt(P("km"), P("kr" + sb), P("mk", 0, 128), A_.mult), ["kr" + sb, ("mk", 0, 128)], ["km"])
+                    TE(512, lambda e, T, QA=QA: [e.matmul(T[QA][:, 264:280], T.idf[:, :], T.cvf[:, :], True, False), e.matmul(T[QA][:, 264:280], T.km[:, :], T.csf[:, :], False, True)],
+                       ["km", "csf", "idf", "cvf"], [(QA, 264, 280)], 2)
+                    V(8, ts(P("kq"), P(QA, 264, 272), BIG16, BIG16, A_.add, A_.subtract), [(QA, 264, 280)], ["kq"])
+                    V(8, tt(P("kd"), P(QA, 272, 280), P("kq"), A_.subtract), [(QA, 264, 280), "kq"], ["kd"])
+                    V(8, tc(P("ofi" + sb), P("kd")), ["kd"], ["ofi" + sb])
+                else:
+                  S(128, lambda e, T, sb=sb, QA=QA: e.activation(T["ot" + sb][:, :], T[QA][:, 0:128], F_.Copy), [(QA, 0, 128)], ["ot" + sb])
+                  TE(128, lambda e, T, sb=sb, QA=QA: [e.matmul(T[QA][:, 128:256], T["ot" + sb][:, :], T.boi[:, :], True, True)], ["ot" + sb, "boi"], [(QA, 128, 256)])
+                  V(128, tt(P("mt" + sb), P("mk", 0, 128), P(QA, 128, 256), A_.mult), ["mk", (QA, 128, 256)], ["mt" + sb])
+                  TE(128, lambda e, T, sb=sb, QA=QA: [e.matmul(T[QA][:, 264:272], T["mt" + sb][:, :], T.cs[:, 0:8], True, False), e.matmul(T[QA][:, 264:272], T.idb[:, :], T.cv[:, 0:8], False, True)],
+                   ["mt" + sb, "cs", "idb", "cv"], [(QA, 264, 272)], 2)
+                  V(64, tc(P("ofi" + sb), P(QA, 264, 272)), [(QA, 264, 272)], ["ofi" + sb])
+                h0, h1 = 128 * b, 128 * b + 128
+                V(270, lambda e, T, sb=sb, o=o, h0=h0, h1=h1: e.tensor_tensor(T.yi[:, h0:h1], T.hh[:, o:o + 2048].indirect(T["ofi" + sb][:, :]), T.zz[:, h0:h1], A_.add),
+                  [("hh", o, o + 2048), "ofi" + sb, ("zz", h0, h1)], [("yi", h0, h1)])
+                V(128, ts(P("y2", h0, h1), P("yi", h0, h1), 1, None, A_.arith_shift_right), [("yi", h0, h1)], [("y2", h0, h1)])
+            else:
+                h0, h1 = 128 * b, 128 * b + 128
+                V(128, tc(P("out" + sb), P(QD, 0, 128)), [(QD, 0, 128)], ["out" + sb])
+                S(128, lambda e, T, sb=sb, h0=h0, h1=h1: e.activation(T["zo" + sb][:, :], T.zz[:, h0:h1], F_.Copy), [("zz", h0, h1)], ["zo" + sb])
+                ops.append(dict(q="Y", c=0.1, fn=("yz", h0, h1, "zo" + sb, "o0" + sb), rd=R(["zo" + sb]), wr=[], n=0, late=2.0))
+                ops.append(dict(q="Y", c=0.1, fn=("yl", h0, h1, "out" + sb, "o1" + sb), rd=R(["out" + sb]), wr=[], n=0, late=2.0))
+        tag(ops, first, TAIL)
+        if t < RO - 1:
+            TE(128, lambda e, T: [e.matmul(T.q0[:, 408:409], T.ones[:, 0:128], T.ms1[:, 128:129], True, False), e.matmul(T.q0[:, 408:409], T.ones[:, 0:128], T.ms0[:, 128:129], False, True)],
+               ["ones", ("ms0", 128, 129), ("ms1", 128, 129)], [("q0", 408, 409)], 2)
+            V(1, ts(P("ei"), P("q0", 408, 409), -1.0, 2048.0, A_.mult, A_.add), [("q0", 408, 409)], ["ei"])
+            V(1, ts(P("ea"), P("ei"), 7, None, A_.bitwise_and), ["ei"], ["ea"])
+            V(1, tt(P("thr", t + 1, t + 2), P("li", t + 1, t + 2), P("ea"), A_.add), ["li", "ea"], [("thr", t + 1, t + 2)])
+            V(1, ts(P("nth", t + 1, t + 2), P("thr", t + 1, t + 2), -1.0, 0.5, A_.mult, A_.add), [("thr", t + 1, t + 2)], [("nth", t + 1, t + 2)])
+            TE(16 * 64, lambda e, T: [e.matmul(T.q2[:, 416:432], T.wr[:, 128 * r:128 * r + 128], T.xl[:, r::16], r == 0, r == 15) for r in range(16)], ["wr", "xl"], [("q2", 416, 432)], 16)
+            V(64, tc(P("uw"), P("q2", 416, 432)), [("q2", 416, 432)], ["uw"])
+            V(64, ts(P("u15"), P("uw"), 15, None, A_.bitwise_and), ["uw"], ["u15"])
+            V(64, tt(P("uv"), P("u15"), P("cvs"), A_.add), ["u15", "cvs"], ["uv"])
+            V(64, tc(P("ofs"), P("uv")), ["uv"], ["ofs"])
+            for b in (1, 0):
+                V(540, lambda e, T, b=b: e.tensor_copy(T.xs[:, :].indirect(T.ofs[:, 8 * b:8 * b + 8]), T.y2[:, 128 * b:128 * b + 128]),
+                  [("y2", 128 * b, 128 * b + 128), "ofs"], ["xs"])
+    return ops
+
+
+def tag(ops, first, b):
+    for op in ops[first:]:
+        op["b"] = b
+
+
+def gat(add, dst, c0, c1, off, ob, win=("xs", 0, 4096), q="VS"):
+    def fn(e, T, scalar):
+        src = T[win[0]][:, win[1]:win[2]].indirect(off(T))
+        return [e.activation(T[dst][:, c0:c1], src, F_.Copy) if scalar else e.tensor_copy(T[dst][:, c0:c1], src)]
+    n = c1 - c0
+    add(q, {"V": 0.06 + n * 1.56 * CYC, "S": 0.075 + n * 1.56 * CYC}, fn, [win, ob], [(dst, c0, c1)], 1, 0.0, True)
+
+
+def held(add, c0, c1, t):
+    def fn(e, T, scalar):
+        if scalar:
+            return [e.activation(T.hb[:, c0:c1], T.mm[:, c0:c1], F_.Sign, bias=T.nth[:, t:t + 1])]
+        return [e.tensor_scalar(T.hb[:, c0:c1], T.mm[:, c0:c1], T.thr[:, t:t + 1], 0.5, A_.is_ge, A_.subtract)]
+    n = c1 - c0
+    add("VS", {"V": 0.02 + n * 0.5 * CYC, "S": 0.065 + n * CYC}, fn, [("mm", c0, c1), ("thr", t, t + 1), ("nth", t, t + 1)], [("hb", c0, c1)], 1, 0.0, True)
+
+
+def link(ops):
+    hist = {}
+    for k, op in enumerate(ops):
+        deps, order = set(), set()
+        acc = [(r, False) for r in op["rd"]] + [(w, True) for w in op["wr"]]
+        for (bn, a, z), wr in acc:
+            ps = SCRATCH[bn][0] == "psum"
+            for (a2, z2, k2, w2) in hist.get(bn, []):
+                if k2 == k:
+                    continue
+                over = a < z2 and a2 < z
+                if ps:
+                    same = op["q"] == ops[k2]["q"]
+                    if not same:
+                        deps.add(k2)
+                    elif over and w2 and op["q"] != "T":
+                        deps.add(k2)
+                    else:
+                        order.add(k2)
+                elif over and (wr or w2):
+                    if w2:
+                        deps.add(k2)
+                    elif op["q"] == ops[k2]["q"] and len(op["q"]) == 1:
+                        order.add(k2)
+                    else:
+                        deps.add(k2)
+        for (bn, a, z), wr in acc:
+            h = hist.setdefault(bn, [])
+            if wr and SCRATCH[bn][0] != "psum":
+                h[:] = [x for x in h if not (a <= x[0] and x[1] <= z)]
+            if SCRATCH[bn][0] == "psum":
+                h[:] = [x for x in h if not (x[2] in deps and (ops[x[2]]["q"] != op["q"] or (a <= x[0] and x[1] <= z)))]
+            h.append((a, z, k, wr))
+        if op.get("after") is not None:
+            for k2 in range(k):
+                if ops[k2].get("send", (None,))[:2] == op["after"]:
+                    order.add(k2)
+        op["deps"], op["order"] = deps, order - deps
+
+
+LAT = 0.08
+
+
+def schedule(ops, bias=0.0, jit=None):
+    n = len(ops)
+    succ = [[] for _ in range(n)]
+    left = [0] * n
+    cost = [op["c"] if isinstance(op["c"], dict) else {q: op["c"] for q in op["q"]} for op in ops]
+    for k, op in enumerate(ops):
+        for d in op["deps"] | op["order"]:
+            succ[d].append(k)
+            left[k] += 1
+    prio = [0.0] * n
+    for k in range(n - 1, -1, -1):
+        op = ops[k]
+        prio[k] = min(cost[k].values()) + op["late"] + LAT + max([prio[s] for s in succ[k]], default=0.0)
+    prio = [prio[k] + (bias if ops[k].get("b", TAIL) != TAIL else 0.0) + (jit[k] if jit is not None else 0.0) for k in range(n)]
+    free = {"V": 0.0, "S": 0.0, "T": 0.0, "G": 0.0, "Y": 0.0, "E": 0.0}
+    end, est = [None] * n, [0.0] * n
+    ready = [k for k in range(n) if left[k] == 0]
+    seq = []
+    while ready:
+        cands = []
+        for k in ready:
+            f, s, q = min((max(est[k], free[q]) + cost[k][q], max(est[k], free[q]), q) for q in ops[k]["q"])
+            cands.append((s, -prio[k], k, q))
+        first = min(cands)[0]
+        s, p, k, q = min((x for x in cands if x[0] <= first + SLACK), key=lambda x: (x[1], x[0], x[3]))
+        op = ops[k]
+        ready.remove(k)
+        op["at"], op["on"], op["cost"] = s, q, cost[k][q]
+        end[k] = s + cost[k][q] + op["late"]
+        if q != "E":
+            free[q] = s + cost[k][q]
+        seq.append(k)
+        for x in succ[k]:
+            left[x] -= 1
+            est[x] = max(est[x], end[k] + (LAT if k in ops[x]["deps"] else 0.0))
+            if left[x] == 0:
+                ready.append(x)
+    return seq, max(end)
+
+
+SLACK = 0.0
+PLAN = {}
+
+
+def plan():
+    if not PLAN:
+        ops = build()
+        link(ops)
+        seq, total = schedule(ops, 8.0)
+        PLAN["ops"], PLAN["seq"], PLAN["total"] = ops, seq, total
+    return PLAN["ops"], PLAN["seq"]
+
+
+def bits(topo, src, dst):
+    return sum(1 << e for e in topo.engines(src, dst)[:NE])
+
+
+def helper(topo, core, dst):
+    for c in topo.cores_of(core):
+        if c != core and topo.die(c) == topo.die(core) and topo.may_write(c, dst):
+            return c
+    return None
+
+
+def send(g, T, topo, core, dst, out, src, rsem):
+    rid, pid = topo.addr(dst, core)
+    (ob, o0, o1), (ib, i0, i1) = at(out), at(src)
+    g.remote_dma(out_ap=T[ob][:, o0:o1], in_ap=T[ib][:, i0:i1], remote_sem=T.sem[rsem], local_sem=T.sem["lsem"], pid=pid, routing_id=rid, dma_engine_mask=bits(topo, core, dst))
+
+
+def rank_program(g, core, T, topo):
+    rank = T.rank_of(core)
+    if rank is None:
+        for r, c in enumerate(T.cores):
+            dst = T.cores[(r + HOPS[1]) % N]
+            if not topo.may_write(c, dst) and helper(topo, c, dst) == core:
+                for t in range(1, RO):
+                    g.wait_ge(T.sem["h%d" % t], NE)
+                    send(g, T, topo, core, dst, "land%d1" % t, "rel%d" % t, "a%d1" % t)
+                g.wait_ge(T.sem["lsem"], NE * (RO - 1))
+        return
+    ops, seq = plan()
+    eng = {"V": g.vector, "S": g.scalar, "T": g.tensor, "G": g, "Y": g.sync}
+    semn = {"V": "sV", "S": "sS", "T": "sT", "G": "sG"}
+    g.sync.dma_start(T.xs[:, :], T.field[:, :]).then_inc(T.sem["dx"], 16)
+    g.scalar.dma_start(T.l0[:, :], T.tube[:, :]).then_inc(T.sem["dt"], 16)
+    g.scalar.dma_start(T.wi[:, :], T.wt[:, :]).then_inc(T.sem["dw"], 16)
+    g.scalar.dma_start(T.ki[:, :], T.kn[:, :]).then_inc(T.sem["dk"], 16)
+    g.scalar.dma_start(T.li[:, :], T.lim[:, :]).then_inc(T.sem["dl"], 16)
+    count = {q: 0 for q in "VSTG"}
+    known = {q: {} for q in "VSTGY"}
+    done, snap = {}, {}
+    sends = 0
+    outs = []
+    for k in seq:
+        op = ops[k]
+        q = op["on"]
+        if q == "E":
+            done[k] = op["fn"]
+            snap[k] = {}
+            continue
+        e = eng[q]
+        need = {}
+        for d in sorted(op["deps"]):
+            if d in done:
+                s, v = done[d]
+                if known[q].get(s, 0) < v and need.get(s, (0, 0))[0] < v:
+                    need[s] = (v, d)
+        for s in sorted(need):
+            v, d = need[s]
+            if any(snap[d2].get(s, 0) >= v for s2, (v2, d2) in need.items() if s2 != s):
+                continue
+            e.wait_ge(T.sem[s], v)
+        for s, (v, d) in need.items():
+            kn_ = known[q]
+            kn_[s] = max(kn_.get(s, 0), v)
+            for s2, v2 in snap[d].items():
+                kn_[s2] = max(kn_.get(s2, 0), v2)
+        snap[k] = dict(known[q])
+        if op.get("send"):
+            t, b, nb = op["send"]
+            dst = T.cores[(rank + HOPS[b]) % N]
+            if topo.may_write(core, dst):
+                send(g, T, topo, core, dst, "land%d%d" % (t + 1, b), nb, "a%d%d" % (t + 1, b))
+            else:
+                send(g, T, topo, core, helper(topo, core, dst), "rel%d" % (t + 1), nb, "h%d" % (t + 1))
+            sends += 1
+        elif q == "Y":
+            o, h0, h1, src, sm = op["fn"]
+            e.dma_start(T[o][:, h0:h1], T[src][:, :]).then_inc(T.sem[sm], 16)
+            outs.append(sm)
+        else:
+            ins = op["fn"](e, T, q == "S") if op.get("gat") else op["fn"](e, T)
+            for x in ins:
+                x.then_inc(T.sem[semn[q]], 1)
+            count[q] += len(ins)
+            done[k] = (semn[q], count[q])
+    for sm in outs:
+        g.sync.wait_ge(T.sem[sm], 16)
+    for q in "VSTG":
+        if count[q]:
+            g.sync.wait_ge(T.sem[semn[q]], count[q])
+    g.wait_ge(T.sem["lsem"], NE * sends)

@@ -372,7 +372,7 @@ def link(ops):
         op["deps"], op["order"] = deps, order - deps
 
 
-LAT = 0.08
+LAT = 0.17
 
 
 def schedule(ops, bias=0.0, jit=None):
@@ -417,13 +417,22 @@ def schedule(ops, bias=0.0, jit=None):
 
 SLACK = 0.0
 PLAN = {}
+ABC = "0123456789abcdefghijklmnopqrstuvwxyzABCDEFGHIJKLMNOPQRSTUVWXYZ"
+SHIFT = "Hn5HSB0sWoYXui7RA78nABE8EBZzIOZKC14QtTAQZZaTN8ozoDTEzE05yVeOQZTZZTTDOTTMLTTHlTihqMt32TxTFszH3qLsQnMCTxTbAC1AAFnSIh7T43eCeAEDRKyLTxPZVryJAGukDAHffVZZLQcXxUWtpyink8jZVuC9PQZdHZZYodZLCzvutVWZmoQVsHZBZZcsZmjUkRZdUttAmPX5xZAZPi05ZC01Q3YEd19aQtdyB7qdlI8YjKVUUbxYZfYwN3u6TRLDsNYMG4uZV0fVVM0xg0vEdcJeubm2Goyb0M3bst0DjWRnRMOCj0KnfOqXV10gdDjq0yiulFSPO2SQKX5ZOZnOPQCbXOlanw5o5fpv580Sa5u5g7f1v0yRKScQDoQFtpIZJrxANUysEuTcwZUZkQZYJiMzqZZWObdDJzmspg66EvM7moZ5NwWF7HZfCr6kaZXeBOjh0QpSoyBvmOq0Emh85KXNZeZUaLg66d6l6w6666n60000KdyR16081R6K8c03e0WOiyooMCBxS0D7MpMAQTMFK4evm4ZIFZLZP0JE1p600jPPPczs03d9C0yhJJZobdjNaHo2hP9KvBFDkZJiZbTZTuLBOQWSTuYR40jcBjzkdcKZOkk7djSt00O7pBt8hXyHWUWFRdWzZ"
+PLACE = "**VV**SVVSS***VV*SSS*VSV*VS*SVSSS*VVVSS*VVS**VVSVV**SVSSSVS**S**VSV*SV*SV**V*VV*"
 
 
 def plan():
     if not PLAN:
         ops = build()
         link(ops)
-        seq, total = schedule(ops, 8.0)
+        both = [op for op in ops if len(op["q"]) > 1]
+        if len(SHIFT) == len(ops) and len(PLACE) == len(both):
+            for op, p in zip(both, PLACE):
+                op["q"] = op["q"] if p == "*" else p
+            seq, total = schedule(ops, 0.0, [(ABC.index(x) - 31) * 0.12 for x in SHIFT])
+        else:
+            seq, total = schedule(ops, 8.0)
         PLAN["ops"], PLAN["seq"], PLAN["total"] = ops, seq, total
     return PLAN["ops"], PLAN["seq"]
 

from concourse.mybir import dt, AluOpType, ActivationFunctionType

N, RO, TU, BL = 8, 4, 256, 128
HOPS = [4, 1]
NE = 8
A_ = AluOpType
F_ = ActivationFunctionType
BIG = 1.5 * 2.0 ** 35

SCRATCH = {}


def buf(name, cols, dtype, where="sbuf"):
    SCRATCH[name] = (where, [128, cols], dtype)


for _n in ("xs", "gg", "mm", "hb", "hh", "aa"):
    buf(_n, 4096, "bfloat16")
buf("l0", 256, "int32"); buf("lo0", 256, "uint16")
buf("rel", BL * 3, "uint16"); buf("land", BL * 6, "uint16"); buf("nb", BL * 6, "uint16")
PART = {}
for _t in range(1, RO):
    PART["rel%d" % _t] = ("rel", BL * (_t - 1))
    for _b in (0, 1):
        PART["land%d%d" % (_t, _b)] = ("land", BL * (2 * _t - 2 + _b))
        PART["nb%d%d" % (_t, _b)] = ("nb", BL * (2 * _t - 2 + _b))


def at(name, a=0, b=BL):
    n, o = PART[name]
    return n, o + a, o + b


for _b in (0, 1):
    for _n, _c, _d in (("lf", 128, "float32"), ("lp", 64, "float32"), ("lq", 128, "float32"), ("sk", 1024, "float32"),
                       ("ok", 128, "bfloat16"), ("ms", 136, "bfloat16"), ("ofm", 16, "uint16"), ("zt", 128, "bfloat16"),
                       ("rr", 128, "float32"), ("ww", 128, "float32"), ("ci", 128, "int32"), ("cc", 128, "int32"),
                       ("ofc", 128, "uint16"), ("ks", 128, "float32"), ("kr", 128, "float32"), ("oh", 128, "bfloat16"),
                       ("ot", 128, "bfloat16"), ("pb", 128, "float32"), ("mt", 128, "bfloat16"), ("ofi", 8, "uint16"),
                       ("rp", 128, "int32"), ("rv", 128, "int32"), ("rest", 128, "float32"), ("out", 128, "float32"),
                       ("zo", 128, "float32")):
        buf(_n + str(_b), _c, _d)
for _n, _c, _d in (("xl", 256, "bfloat16"), ("zz", 256, "bfloat16"), ("yi", 256, "int32"), ("y2", 256, "int32"),
                   ("ofs", 16, "uint16"), ("uw", 16, "int32"), ("u15", 16, "int32"), ("uv", 16, "int32"),
                   ("ei", 1, "int32"), ("ea", 1, "int32"), ("thr", 4, "float32"), ("nth", 4, "float32"),
                   ("bm", 128, "float32"), ("km", 128, "float32"), ("kq", 8, "float32"), ("kd", 8, "int32"),
                   ("csf", 16, "float32"), ("cvf", 16, "float32"),
                   ("wi", 1, "int32"), ("ki", 1, "int32"), ("li", 4, "int32"),
                   ("pc", 1, "int32"), ("pi", 1, "int32"), ("pg", 1, "int32"), ("row", 128, "int32"), ("r15", 128, "int32"),
                   ("r16", 128, "int32"), ("cols", 24, "float32"), ("tq", 128, "float32"),
                   ("bo", 128, "bfloat16"), ("qp", 128, "bfloat16"),
                   ("mk", 136, "bfloat16"), ("idb", 128, "bfloat16"), ("nid", 128, "bfloat16"), ("idf", 128, "float32"),
                   ("r0f", 128, "float32"), ("bom", 136, "bfloat16"), ("boi", 128, "bfloat16"), ("wb", 128, "bfloat16"),
                   ("ind", 2048, "bfloat16"), ("wr", 2048, "bfloat16"), ("sh", 1920, "float32"), ("ex", 2048, "bfloat16"),
                   ("ones", 2048, "bfloat16"), ("rst", 1024, "bfloat16"), ("rs2", 128, "float32"), ("kc", 128, "bfloat16"),
                   ("irow", 128, "bfloat16"), ("cr", 16, "float32"), ("cw", 16, "float32"), ("cv", 16, "bfloat16"),
                   ("cvs", 16, "int32"), ("cs", 16, "bfloat16"), ("g8", 8, "bfloat16"), ("koi", 8, "int32"), ("kof", 8, "uint16")):
    buf(_n, _c, _d)
for _n in range(8):
    buf("q%d" % _n, 512, "float32", "psum")

SEMAPHORES = ["sV", "sS", "sT", "sG", "dx", "dt", "dw", "dk", "dl", "lsem", "o00", "o01", "o10", "o11"]
SEMAPHORES += ["a%d%d" % (_t, _b) for _t in range(1, RO) for _b in (0, 1)] + ["h%d" % _t for _t in range(1, RO)]

BIG16 = 1.5 * 2.0 ** 27
TAIL = 0
CH = 64

CYC, TEC = 0.00083, 0.000417


def build():
    ops = []

    def add(q, cost, fn, rd, wr, n=1, late=0.0, gat=False):
        ops.append(dict(q=q, c=cost, fn=fn, rd=rd, wr=wr, n=n, late=late, gat=gat))

    def whole(*names):
        return [(x, 0, SCRATCH[x][1][1]) for x in names]

    def R(x):
        return [y if isinstance(y, tuple) else at(y) if y in PART else whole(y)[0] for y in x]

    def V(cyc, fn, rd, wr):
        add("V", max(64, cyc) * CYC + 0.02, lambda e, T: [fn(e, T)], R(rd), R(wr))

    def S(cyc, fn, rd, wr):
        add("S", cyc * CYC + 0.065, lambda e, T: [fn(e, T)], R(rd), R(wr))

    def TE(cyc, fn, rd, wr, n=1):
        add("T", cyc * TEC + 0.03, fn, R(rd), R(wr), n)

    def GP(cyc, fn, rd, wr):
        add("G", 0.17 + cyc * CYC, lambda e, T: [fn(e, T)], R(rd), R(wr))

    def ev(sem, val, buf, late):
        add("E", 0.0, (sem, val), [], R([buf]), 0, late)

    def ts(out, in0, s1, s2, *op):
        return lambda e, T: e.tensor_scalar(out(T), in0(T), s1(T) if callable_(s1) else s1, s2(T) if callable_(s2) else s2, *op)

    def callable_(x):
        return not isinstance(x, (int, float)) and x is not None

    def tt(out, a, b, op):
        return lambda e, T: e.tensor_tensor(out(T), a(T), b(T), op)

    def tc(out, a):
        return lambda e, T: e.tensor_copy(out(T), a(T))

    def P(name, a=None, b=None):
        if name in PART:
            name, a, b = at(name) if a is None else at(name, a, b)
        return (lambda T: T[name][:, :]) if a is None else (lambda T: T[name][:, a:b])

    def col(j):
        return P("cols", j, j + 1)

    ev("dx", 16, "xs", 6.0); ev("dt", 16, "l0", 3.0); ev("dw", 16, "wi", 2.5); ev("dk", 16, "ki", 2.5); ev("dl", 16, "li", 2.5)
    GP(2, lambda e, T: e.iota(T.pc[:, :], [[0, 1]], 0, 1), [], ["pc"])
    GP(256, lambda e, T: e.iota(T.row[:, :], [[1, 128]], 0, 0), [], ["row"])
    GP(16, lambda e, T: e.iota(T.koi[:, :], [[16, 8]], 15, 0), [], ["koi"])
    GP(32, lambda e, T: e.iota(T.cr[:, :], [[1, 16]], 0, 0, allow_small_or_imprecise_dtypes=True), [], ["cr"])
    GP(32, lambda e, T: e.iota(T.cw[:, :], [[0, 4], [16, 4]], 0, 0, allow_small_or_imprecise_dtypes=True), [], ["cw"])
    V(1024, lambda e, T: e.memset(T.ones[:, :], 1.0), [], ["ones"])
    GP(4096, lambda e, T: e.affine_select(T.ex[:, :], T.ones[:, :], [[-1, 128], [0, 16]], A_.is_equal, 0.0, 0, 1), ["ones"], ["ex"])
    V(512, lambda e, T: e.memset(T.rst[:, :], 0.0), [], ["rst"])
    V(64, lambda e, T: e.memset(T.rst[:, 0::16], 1024.0), [], ["rst"])
    V(128, lambda e, T: e.memset(T.rs2[:, :], 0.0), [], ["rs2"])
    V(64, lambda e, T: e.memset(T.rs2[:, 0::16], 1048576.0), [], ["rs2"])
    V(64, lambda e, T: e.memset(T.kc[:, :], 0.5), [], ["kc"])
    V(64, lambda e, T: e.memset(T.kc[0:1, :], -2048.0), [], ["kc"])
    for b in (0, 1):
        V(64, lambda e, T, b=b: e.memset(T["sk%d" % b][:, 0:64], 0.0), [], [("sk%d" % b, 0, 64)])
    V(1, ts(P("pi"), P("pc"), 15, None, A_.bitwise_and), ["pc"], ["pi"])
    V(1, ts(P("pg"), P("pc"), 112, None, A_.bitwise_and), ["pc"], ["pg"])
    V(1, tc(col(0), P("pi")), ["pi"], [("cols", 0, 1)])
    V(1, tc(col(1), P("pg")), ["pg"], [("cols", 1, 2)])
    V(1, ts(col(2), P("pi"), 1.0, None, A_.is_ge), ["pi"], [("cols", 2, 3)])
    V(1, ts(col(3), P("pi"), 15.0, None, A_.is_ge), ["pi"], [("cols", 3, 4)])
    V(1, ts(col(4), col(2), 20.75, -20.0, A_.mult, A_.add), [("cols", 2, 3)], [("cols", 4, 5)])
    V(1, ts(col(5), P("pi"), 16.0, None, A_.mult), ["pi"], [("cols", 5, 6)])
    V(1, ts(col(6), P("pg"), 0.0625, None, A_.mult), ["pg"], [("cols", 6, 7)])
    V(1, tc(col(7), P("wi")), ["wi"], [("cols", 7, 8)])
    V(1, ts(col(8), P("ki"), 8.0, 2047.5, A_.mult, A_.add), ["ki"], [("cols", 8, 9)])
    V(1, tc(col(10), P("ki")), ["ki"], [("cols", 10, 11)])
    V(1, ts(col(9), P("ki"), col(10), -64.0, A_.mult, A_.mult), ["ki", ("cols", 10, 11)], [("cols", 9, 10)])
    V(1, tc(P("thr", 0, 1), P("li", 0, 1)), ["li"], [("thr", 0, 1)])
    V(1, ts(P("nth", 0, 1), P("li", 0, 1), -1.0, 0.5, A_.mult, A_.add), ["li"], [("nth", 0, 1)])
    V(128, ts(P("r15"), P("row"), 15, None, A_.bitwise_and), ["row"], ["r15"])
    V(128, ts(P("r16"), P("row"), 112, None, A_.bitwise_and), ["row"], ["r16"])
    c = lambda j: ("cols", j, j + 1)
    V(128, ts(P("bo"), P("r16"), col(1), None, A_.is_equal), ["r16", c(1)], ["bo"])
    V(128, ts(P("tq"), P("r15"), 1.0, None, A_.add), ["r15"], ["tq"])
    V(256, tt(P("qp"), P("tq"), P("bo"), A_.mult), ["tq", "bo"], ["qp"])
    for i in range(16):
        V(64, ts(P("ind", 128 * i, 128 * i + 128), P("qp"), float(i + 1), None, A_.is_equal), ["qp"], [("ind", 128 * i, 128 * i + 128)])
    V(128, ts(P("mk", 0, 128), P("r15"), col(0), None, A_.is_equal), ["r15", c(0)], [("mk", 0, 128)])
    V(1, lambda e, T: e.memset(T.mk[:, 128:136], 1.0), [], [("mk", 128, 136)])
    V(128, ts(P("bom", 0, 128), P("bo"), col(2), None, A_.mult), ["bo", c(2)], [("bom", 0, 128)])
    V(1, tc(P("bom", 128, 129), col(3)), [c(3)], [("bom", 128, 129)])
    V(64, ts(P("boi"), P("bo"), col(0), None, A_.mult), ["bo", c(0)], ["boi"])
    V(64, ts(P("wb"), P("bo"), col(7), None, A_.mult), ["bo", c(7)], ["wb"])
    V(256, tt(P("idb"), P("bo"), P("mk", 0, 128), A_.mult), ["bo", ("mk", 0, 128)], ["idb"])
    S(128, lambda e, T: e.activation(T.nid[:, :], T.idb[:, :], F_.Copy, scale=-1.0), ["idb"], ["nid"])
    S(128, lambda e, T: e.activation(T.idf[:, :], T.idb[:, :], F_.Copy), ["idb"], ["idf"])
    V(128, ts(P("r0f"), P("qp"), 1.0, None, A_.is_equal), ["qp"], ["r0f"])
    V(128, tc(P("irow"), P("r15")), ["r15"], ["irow"])
    V(64, ts(P("cs", 0, 8), P("cr", 0, 8), col(6), None, A_.is_equal), ["cr", c(6)], [("cs", 0, 8)])
    V(64, ts(P("cs", 8, 16), P("cr", 0, 8), col(6), 64.0, A_.is_equal, A_.mult), ["cr", c(6)], [("cs", 8, 16)])
    V(64, ts(P("g8"), P("cr", 0, 8), col(6), 16.0, A_.is_equal, A_.mult), ["cr", c(6)], ["g8"])
    V(64, ts(P("cv", 0, 8), P("cr", 0, 8), 256.0, col(5), A_.mult, A_.add), ["cr", c(5)], [("cv", 0, 8)])
    V(64, ts(P("cv", 8, 16), P("cw", 0, 8), col(0), None, A_.add), ["cw", c(0)], [("cv", 8, 16)])
    V(64, ts(P("cvs"), P("cr"), 256.0, col(5), A_.mult, A_.add), ["cr", c(5)], ["cvs"])
    V(64, tc(P("kof"), P("koi")), ["koi"], ["kof"])
    V(128, ts(P("bm"), P("qp"), 2.0, col(2), A_.is_ge, A_.mult), ["qp", c(2)], ["bm"])
    for y in range(1, 16):
        GP(256, lambda e, T, y=y: e.affine_select(T.sh[:, 128 * (y - 1):128 * y], T.bm[:, :], [[-16, 8], [1, 16]], A_.is_equal, 0.0, -(y + 1), 1), ["bm"], [("sh", 128 * (y - 1), 128 * y)])
    S(2048, lambda e, T: e.activation(T.wr[:, :], T.ind[:, :], F_.Copy, scale=T.cols[:, 7:8]), ["ind", c(7)], ["wr"])
    V(64, ts(P("csf", 0, 8), P("cr", 0, 8), col(6), None, A_.is_equal), ["cr", c(6)], [("csf", 0, 8)])
    V(64, ts(P("csf", 8, 16), P("cr", 0, 8), col(6), None, A_.is_equal), ["cr", c(6)], [("csf", 8, 16)])
    V(64, lambda e, T: e.memset(T.cvf[:, 0:8], -7.5), [], [("cvf", 0, 8)])
    V(64, ts(P("cvf", 8, 16), P("cr", 0, 8), 256.0, col(5), A_.mult, A_.add), ["cr", c(5)], [("cvf", 8, 16)])

    def mm(e, out, l, r, st, sp):
        return e.matmul(out, l, r, st, sp)

    for t in range(RO):
        first = len(ops)
        for b in (1 - TAIL, TAIL):
            tag(ops, first, 1 - b)
            first = len(ops)
            sb = str(b)
            QA, QB, QC, QD = "q%d" % (2 * b), "q%d" % (2 * b + 1), "q%d" % (4 + 2 * b), "q%d" % (5 + 2 * b)
            o = 2048 * b
            if t == 0:
                off = lambda v0, v1, b=b: P("lo0", 128 * b + v0, 128 * b + v1)
                V(128, tc(P("lo0", 128 * b, 128 * b + 128), P("l0", 128 * b, 128 * b + 128)), [("l0", 128 * b, 128 * b + 128)], [("lo0", 128 * b, 128 * b + 128)])
                ob = ("lo0", 128 * b, 128 * b + 128)
                V(128, tc(P("lf" + sb), P("l0", 128 * b, 128 * b + 128)), [("l0", 128 * b, 128 * b + 128)], ["lf" + sb])
            else:
                ln = "land%d%d" % (t, b)
                ops.append(dict(q="E", c=0.0, fn=("a%d%d" % (t, b), NE), rd=[], wr=R([ln]), n=0, late=4.5 if b else 2.8, after=(t - 1, b)))
                off = lambda v0, v1, ln=ln: P(ln, v0, v1)
                ob = at(ln)
                V(128, tc(P("lf" + sb), P(ln)), [ln], ["lf" + sb])

            for v0 in range(0, 128, CH):
                c0, c1 = o + 16 * v0, o + 16 * (v0 + CH)
                gat(add, "gg", c0, c1, off(v0, v0 + CH), ob)
                V((c1 - c0) // 2, lambda e, T, c0=c0, c1=c1: e.tensor_tensor_scan(T.mm[:, c0:c1], T.rst[:, 0:c1 - c0], T.gg[:, c0:c1], 0.0, A_.add, A_.min),
                  ["rst", ("gg", c0, c1)], [("mm", c0, c1)])
                held(add, c0, c1, t)
                TE(16 * 64, lambda e, T, v0=v0, c0=c0, c1=c1, QA=QA, CH=CH: [e.matmul(T[QA][:, v0:v0 + CH], T.ind[:, 128 * i:128 * i + 128], T.hb[:, c0 + i:c1:16], i == 0, i == 15) for i in range(16)],
                   ["ind", ("hb", c0, c1)], [(QA, v0, v0 + CH)], 16)
            S(128, lambda e, T, sb=sb: e.activation(T["lq" + sb][:, :], T["lf" + sb][:, :], F_.Identity, bias=T.cols[:, 9:10], scale=16.0), ["lf" + sb, c(9)], ["lq" + sb])
            S(64, lambda e, T, sb=sb, QD=QD: e.activation(T[QD][:, 0:64], T["lf" + sb][:, 0:64], F_.Copy, scale=4096.0), ["lf" + sb], [(QD, 0, 64)])
            V(64, tt(P("lp" + sb), P("lf" + sb, 64, 128), P(QD, 0, 64), A_.add), ["lf" + sb, (QD, 0, 64)], ["lp" + sb])
            for Q, y0, y1 in ((QC, 1, 8), (QD, 8, 16)):
                n = y1 - y0
                TE(n * 256, lambda e, T, Q=Q, y0=y0, y1=y1, sb=sb: [e.matmul(T[Q][:, 64 * (y - y0):64 * (y - y0) + 64], T.sh[:, 128 * (y - 1):128 * y], T["lp" + sb][:, :], True, True) for y in range(y0, y1)],
                   ["sh", "lp" + sb], [(Q, 0, 64 * n)], n)
                S(64 * n, lambda e, T, Q=Q, n=n, y0=y0, sb=sb: e.activation(T["sk" + sb][:, 64 * y0:64 * y0 + 64 * n], T[Q][:, 0:64 * n], F_.Copy), [(Q, 0, 64 * n)], [("sk" + sb, 64 * y0, 64 * y0 + 64 * n)])
            V(128, ts(P("ok" + sb), P(QA, 0, 128), col(4), None, A_.is_ge), [(QA, 0, 128), c(4)], ["ok" + sb])
            TE(129, lambda e, T, sb=sb, QA=QA: [e.matmul(T[QA][:, 128:257], T["ok" + sb][:, :], T.bom[:, 0:129], True, True)], ["ok" + sb, ("bom", 0, 129)], [(QA, 128, 257)])
            V(129, tt(P("ms" + sb, 0, 129), P("mk", 0, 129), P(QA, 128, 257), A_.mult), ["mk", (QA, 128, 257)], [("ms" + sb, 0, 129)])
            TE(128, lambda e, T, sb=sb, QA=QA: [e.matmul(T[QA][:, 264:280], T["ms" + sb][:, 0:128], T.cs[:, :], True, False), e.matmul(T[QA][:, 264:280], T.idb[:, :], T.cv[:, :], False, True)],
               [("ms" + sb, 0, 129), "cs", "idb", "cv"], [(QA, 264, 280)], 2)
            V(64, tc(P("ofm" + sb), P(QA, 264, 280)), [(QA, 264, 280)], ["ofm" + sb])
            gat(add, "xl", 128 * b, 128 * b + 128, P("ofm" + sb, 0, 8), ("ofm" + sb, 0, 16), ("gg", o, o + 2048))
            gat(add, "zz", 128 * b, 128 * b + 128, P("ofm" + sb, 0, 8), ("ofm" + sb, 0, 16), ("mm", o, o + 2048))
            TE(192, lambda e, T, b=b, QB=QB: [e.matmul(T[QB][:, 0:128], T.wb[:, :], T.xl[:, 128 * b:128 * b + 128], True, False), e.matmul(T[QB][:, 0:128], T.kc[0:2, :], T.ones[0:2, 0:128], False, True)],
               ["wb", ("xl", 128 * b, 128 * b + 128), "kc", "ones"], [(QB, 0, 128)], 2)
            V(128, ts(P("rr" + sb), P(QB, 0, 128), BIG, BIG, A_.add, A_.subtract), [(QB, 0, 128)], ["rr" + sb])
            V(128, tt(P("ww" + sb), P(QB, 0, 128), P("rr" + sb), A_.subtract), [(QB, 0, 128), "rr" + sb], ["ww" + sb])
            S(128, lambda e, T, sb=sb, QB=QB: e.activation(T[QB][:, 128:256], T["ww" + sb][:, :], F_.Square, bias=T.cols[:, 8:9]), ["ww" + sb, c(8)], [(QB, 128, 256)])
            V(128, tt(P("ci" + sb), P("lq" + sb), P(QB, 128, 256), A_.add), ["lq" + sb, (QB, 128, 256)], ["ci" + sb])
            V(128, ts(P("cc" + sb), P("ci" + sb), 4, 4095, A_.arith_shift_right, A_.bitwise_and), ["ci" + sb], ["cc" + sb])
            V(128, tc(P("ofc" + sb), P("cc" + sb)), ["cc" + sb], ["ofc" + sb])
            TE(128, lambda e, T, b=b, QD=QD: [e.matmul(T[QD][:, 0:128], T.zz[:, 128 * b:128 * b + 128], T.nid[:, :], True, True)], [("zz", 128 * b, 128 * b + 128), "nid"], [(QD, 0, 128)])
            S(128, lambda e, T, sb=sb, QD=QD: e.activation(T["zt" + sb][:, :], T[QD][:, 0:128], F_.Copy), [(QD, 0, 128)], ["zt" + sb])
            for k in range(4):
                Q = (QC, QD)[k % 2]
                c0, c1 = o + 512 * k, o + 512 * k + 512
                gat(add, "hh", c0, c1, P("ofc" + sb, 32 * k, 32 * k + 32), ("ofc" + sb, 0, 128))
                TE(1024, lambda e, T, Q=Q, c0=c0, c1=c1, k=k, sb=sb: [e.matmul(T[Q][:, :], T["zt" + sb][:, :], T.ex[:, 512 * k:512 * k + 512], True, False), e.matmul(T[Q][:, :], T.idb[:, :], T.hh[:, c0:c1], False, True)],
                   ["zt" + sb, "ex", "idb", ("hh", c0, c1)], [Q], 2)
                S(512, lambda e, T, Q=Q, c0=c0, c1=c1: e.activation(T.aa[:, c0:c1], T[Q][:, :], F_.Abs), [Q], [("aa", c0, c1)])
            V(270, lambda e, T, sb=sb: e.tensor_copy(T["rp" + sb][:, :], T["sk" + sb][:, :].indirect(T["ofm" + sb][:, 8:16])), ["sk" + sb, ("ofm" + sb, 0, 16)], ["rp" + sb])
            V(64, ts(P("rv" + sb, 0, 64), P("rp" + sb, 0, 64), 12, None, A_.arith_shift_right), ["rp" + sb], [("rv" + sb, 0, 64)])
            V(64, ts(P("rv" + sb, 64, 128), P("rp" + sb, 64, 128), 4095, None, A_.bitwise_and), ["rp" + sb], [("rv" + sb, 64, 128)])
            TE(256, lambda e, T, sb=sb, QA=QA: [e.matmul(T[QA][:, 280:408], T.nid[:, :], T["ok" + sb][:, :], True, False), e.matmul(T[QA][:, 280:408], T.ones[0:1, 0:128], T.ones[0:1, 0:128], False, True)],
               ["nid", "ok" + sb, "ones"], [(QA, 280, 408)], 2)
            V(128, tt(P(QA, 0, 128), P("cc" + sb), P(QA, 280, 408), A_.mult), ["cc" + sb, (QA, 280, 408)], [(QA, 0, 128)])
            V(128, tt(P("rest" + sb), P("rv" + sb), P(QA, 0, 128), A_.add), ["rv" + sb, (QA, 0, 128)], ["rest" + sb])
            TE(16 * 64 + 128, lambda e, T, o=o, QB=QB: [e.matmul(T[QB][:, 384:512], T.ones[0:1, 0:128], T.irow[0:1, :], True, False)] +
               [e.matmul(T[QB][:, 384 + i:512:16], T.aa[:, o + i:o + 2048:16], T.g8[:, :], False, i == 15) for i in range(16)],
               ["ones", "irow", ("aa", o, o + 2048), "g8"], [(QB, 384, 512)], 17)
            V(128, lambda e, T, sb=sb, QB=QB: e.tensor_tensor_scan(T["ks" + sb][:, :], T.rs2[:, :], T[QB][:, 384:512], 0.0, A_.add, A_.min), ["rs2", (QB, 384, 512)], ["ks" + sb])
            V(270, lambda e, T, sb=sb: e.tensor_copy(T["kr" + sb][:, :], T["ks" + sb][:, :].indirect(T.kof[:, :])), ["ks" + sb, "kof"], ["kr" + sb])
            V(128, tt(P("oh" + sb), P("kr" + sb), P(QB, 384, 512), A_.is_equal), ["kr" + sb, (QB, 384, 512)], ["oh" + sb])
            TE(128, lambda e, T, sb=sb, QA=QA: [e.matmul(T[QA][:, 0:128], T["oh" + sb][:, :], T.idb[:, :], True, True)], ["oh" + sb, "idb"], [(QA, 0, 128)])
            V(128, tt(P("pb" + sb), P("cc" + sb), P(QA, 0, 128), A_.mult), ["cc" + sb, (QA, 0, 128)], ["pb" + sb])
            TE(512, lambda e, T, sb=sb, QD=QD: [e.matmul(T[QD][:, 0:128], T.idf[:, :], T["rest" + sb][:, :], True, False)], ["idf", "rest" + sb], [(QD, 0, 128)])
            TE(512, lambda e, T, sb=sb, QD=QD: [e.matmul(T[QD][:, 0:128], T.r0f[:, :], T["pb" + sb][:, :], False, True)], ["r0f", "pb" + sb], [(QD, 0, 128)])
            if t < RO - 1:
                nb = "nb%d%d" % (t + 1, b)
                V(128, tc(P(nb), P(QD, 0, 128)), [(QD, 0, 128)], [nb])
                ops.append(dict(q="G", c=1.0, fn=None, rd=R([nb]), wr=[], n=0, late=0.0, send=(t, b, nb)))
                if b == TAIL:
                    V(256, tt(P("km"), P("kr" + sb), P("mk", 0, 128), A_.mult), ["kr" + sb, ("mk", 0, 128)], ["km"])
                    TE(512, lambda e, T, QA=QA: [e.matmul(T[QA][:, 264:280], T.idf[:, :], T.cvf[:, :], True, False), e.matmul(T[QA][:, 264:280], T.km[:, :], T.csf[:, :], False, True)],
                       ["km", "csf", "idf", "cvf"], [(QA, 264, 280)], 2)
                    V(8, ts(P("kq"), P(QA, 264, 272), BIG16, BIG16, A_.add, A_.subtract), [(QA, 264, 280)], ["kq"])
                    V(8, tt(P("kd"), P(QA, 272, 280), P("kq"), A_.subtract), [(QA, 264, 280), "kq"], ["kd"])
                    V(8, tc(P("ofi" + sb), P("kd")), ["kd"], ["ofi" + sb])
                else:
                  S(128, lambda e, T, sb=sb, QA=QA: e.activation(T["ot" + sb][:, :], T[QA][:, 0:128], F_.Copy), [(QA, 0, 128)], ["ot" + sb])
                  TE(128, lambda e, T, sb=sb, QA=QA: [e.matmul(T[QA][:, 128:256], T["ot" + sb][:, :], T.boi[:, :], True, True)], ["ot" + sb, "boi"], [(QA, 128, 256)])
                  V(128, tt(P("mt" + sb), P("mk", 0, 128), P(QA, 128, 256), A_.mult), ["mk", (QA, 128, 256)], ["mt" + sb])
                  TE(128, lambda e, T, sb=sb, QA=QA: [e.matmul(T[QA][:, 264:272], T["mt" + sb][:, :], T.cs[:, 0:8], True, False), e.matmul(T[QA][:, 264:272], T.idb[:, :], T.cv[:, 0:8], False, True)],
                   ["mt" + sb, "cs", "idb", "cv"], [(QA, 264, 272)], 2)
                  V(64, tc(P("ofi" + sb), P(QA, 264, 272)), [(QA, 264, 272)], ["ofi" + sb])
                h0, h1 = 128 * b, 128 * b + 128
                V(270, lambda e, T, sb=sb, o=o, h0=h0, h1=h1: e.tensor_tensor(T.yi[:, h0:h1], T.hh[:, o:o + 2048].indirect(T["ofi" + sb][:, :]), T.zz[:, h0:h1], A_.add),
                  [("hh", o, o + 2048), "ofi" + sb, ("zz", h0, h1)], [("yi", h0, h1)])
                V(128, ts(P("y2", h0, h1), P("yi", h0, h1), 1, None, A_.arith_shift_right), [("yi", h0, h1)], [("y2", h0, h1)])
            else:
                h0, h1 = 128 * b, 128 * b + 128
                V(128, tc(P("out" + sb), P(QD, 0, 128)), [(QD, 0, 128)], ["out" + sb])
                S(128, lambda e, T, sb=sb, h0=h0, h1=h1: e.activation(T["zo" + sb][:, :], T.zz[:, h0:h1], F_.Copy), [("zz", h0, h1)], ["zo" + sb])
                ops.append(dict(q="Y", c=0.1, fn=("yz", h0, h1, "zo" + sb, "o0" + sb), rd=R(["zo" + sb]), wr=[], n=0, late=2.0))
                ops.append(dict(q="Y", c=0.1, fn=("yl", h0, h1, "out" + sb, "o1" + sb), rd=R(["out" + sb]), wr=[], n=0, late=2.0))
        tag(ops, first, TAIL)
        if t < RO - 1:
            TE(128, lambda e, T: [e.matmul(T.q0[:, 408:409], T.ones[:, 0:128], T.ms1[:, 128:129], True, False), e.matmul(T.q0[:, 408:409], T.ones[:, 0:128], T.ms0[:, 128:129], False, True)],
               ["ones", ("ms0", 128, 129), ("ms1", 128, 129)], [("q0", 408, 409)], 2)
            V(1, ts(P("ei"), P("q0", 408, 409), -1.0, 2048.0, A_.mult, A_.add), [("q0", 408, 409)], ["ei"])
            V(1, ts(P("ea"), P("ei"), 7, None, A_.bitwise_and), ["ei"], ["ea"])
            V(1, tt(P("thr", t + 1, t + 2), P("li", t + 1, t + 2), P("ea"), A_.add), ["li", "ea"], [("thr", t + 1, t + 2)])
            V(1, ts(P("nth", t + 1, t + 2), P("thr", t + 1, t + 2), -1.0, 0.5, A_.mult, A_.add), [("thr", t + 1, t + 2)], [("nth", t + 1, t + 2)])
            TE(16 * 64, lambda e, T: [e.matmul(T.q2[:, 416:432], T.wr[:, 128 * r:128 * r + 128], T.xl[:, r::16], r == 0, r == 15) for r in range(16)], ["wr", "xl"], [("q2", 416, 432)], 16)
            V(64, tc(P("uw"), P("q2", 416, 432)), [("q2", 416, 432)], ["uw"])
            V(64, ts(P("u15"), P("uw"), 15, None, A_.bitwise_and), ["uw"], ["u15"])
            V(64, tt(P("uv"), P("u15"), P("cvs"), A_.add), ["u15", "cvs"], ["uv"])
            V(64, tc(P("ofs"), P("uv")), ["uv"], ["ofs"])
            for b in (1, 0):
                V(540, lambda e, T, b=b: e.tensor_copy(T.xs[:, :].indirect(T.ofs[:, 8 * b:8 * b + 8]), T.y2[:, 128 * b:128 * b + 128]),
                  [("y2", 128 * b, 128 * b + 128), "ofs"], ["xs"])
    return ops


def tag(ops, first, b):
    for op in ops[first:]:
        op["b"] = b


def gat(add, dst, c0, c1, off, ob, win=("xs", 0, 4096), q="VS"):
    def fn(e, T, scalar):
        src = T[win[0]][:, win[1]:win[2]].indirect(off(T))
        return [e.activation(T[dst][:, c0:c1], src, F_.Copy) if scalar else e.tensor_copy(T[dst][:, c0:c1], src)]
    n = c1 - c0
    add(q, {"V": 0.06 + n * 1.56 * CYC, "S": 0.075 + n * 1.56 * CYC}, fn, [win, ob], [(dst, c0, c1)], 1, 0.0, True)


def held(add, c0, c1, t):
    def fn(e, T, scalar):
        if scalar:
            return [e.activation(T.hb[:, c0:c1], T.mm[:, c0:c1], F_.Sign, bias=T.nth[:, t:t + 1])]
        return [e.tensor_scalar(T.hb[:, c0:c1], T.mm[:, c0:c1], T.thr[:, t:t + 1], 0.5, A_.is_ge, A_.subtract)]
    n = c1 - c0
    add("VS", {"V": 0.02 + n * 0.5 * CYC, "S": 0.065 + n * CYC}, fn, [("mm", c0, c1), ("thr", t, t + 1), ("nth", t, t + 1)], [("hb", c0, c1)], 1, 0.0, True)


def link(ops):
    hist = {}
    for k, op in enumerate(ops):
        deps, order = set(), set()
        acc = [(r, False) for r in op["rd"]] + [(w, True) for w in op["wr"]]
        for (bn, a, z), wr in acc:
            ps = SCRATCH[bn][0] == "psum"
            for (a2, z2, k2, w2) in hist.get(bn, []):
                if k2 == k:
                    continue
                over = a < z2 and a2 < z
                if ps:
                    same = op["q"] == ops[k2]["q"]
                    if not same:
                        deps.add(k2)
                    elif over and w2 and op["q"] != "T":
                        deps.add(k2)
                    else:
                        order.add(k2)
                elif over and (wr or w2):
                    if w2:
                        deps.add(k2)
                    elif op["q"] == ops[k2]["q"] and len(op["q"]) == 1:
                        order.add(k2)
                    else:
                        deps.add(k2)
        for (bn, a, z), wr in acc:
            h = hist.setdefault(bn, [])
            if wr and SCRATCH[bn][0] != "psum":
                h[:] = [x for x in h if not (a <= x[0] and x[1] <= z)]
            if SCRATCH[bn][0] == "psum":
                h[:] = [x for x in h if not (x[2] in deps and (ops[x[2]]["q"] != op["q"] or (a <= x[0] and x[1] <= z)))]
            h.append((a, z, k, wr))
        if op.get("after") is not None:
            for k2 in range(k):
                if ops[k2].get("send", (None,))[:2] == op["after"]:
                    order.add(k2)
        op["deps"], op["order"] = deps, order - deps


LAT = 0.17


def schedule(ops, bias=0.0, jit=None):
    n = len(ops)
    succ = [[] for _ in range(n)]
    left = [0] * n
    cost = [op["c"] if isinstance(op["c"], dict) else {q: op["c"] for q in op["q"]} for op in ops]
    for k, op in enumerate(ops):
        for d in op["deps"] | op["order"]:
            succ[d].append(k)
            left[k] += 1
    prio = [0.0] * n
    for k in range(n - 1, -1, -1):
        op = ops[k]
        prio[k] = min(cost[k].values()) + op["late"] + LAT + max([prio[s] for s in succ[k]], default=0.0)
    prio = [prio[k] + (bias if ops[k].get("b", TAIL) != TAIL else 0.0) + (jit[k] if jit is not None else 0.0) for k in range(n)]
    free = {"V": 0.0, "S": 0.0, "T": 0.0, "G": 0.0, "Y": 0.0, "E": 0.0}
    end, est = [None] * n, [0.0] * n
    ready = [k for k in range(n) if left[k] == 0]
    seq = []
    while ready:
        cands = []
        for k in ready:
            f, s, q = min((max(est[k], free[q]) + cost[k][q], max(est[k], free[q]), q) for q in ops[k]["q"])
            cands.append((s, -prio[k], k, q))
        first = min(cands)[0]
        s, p, k, q = min((x for x in cands if x[0] <= first + SLACK), key=lambda x: (x[1], x[0], x[3]))
        op = ops[k]
        ready.remove(k)
        op["at"], op["on"], op["cost"] = s, q, cost[k][q]
        end[k] = s + cost[k][q] + op["late"]
        if q != "E":
            free[q] = s + cost[k][q]
        seq.append(k)
        for x in succ[k]:
            left[x] -= 1
            est[x] = max(est[x], end[k] + (LAT if k in ops[x]["deps"] else 0.0))
            if left[x] == 0:
                ready.append(x)
    return seq, max(end)


SLACK = 0.0
PLAN = {}
ABC = "0123456789abcdefghijklmnopqrstuvwxyzABCDEFGHIJKLMNOPQRSTUVWXYZ"
SHIFT = "Hn5HSB0sWoYXui7RA78nABE8EBZzIOZKC14QtTAQZZaTN8ozoDTEzE05yVeOQZTZZTTDOTTMLTTHlTihqMt32TxTFszH3qLsQnMCTxTbAC1AAFnSIh7T43eCeAEDRKyLTxPZVryJAGukDAHffVZZLQcXxUWtpyink8jZVuC9PQZdHZZYodZLCzvutVWZmoQVsHZBZZcsZmjUkRZdUttAmPX5xZAZPi05ZC01Q3YEd19aQtdyB7qdlI8YjKVUUbxYZfYwN3u6TRLDsNYMG4uZV0fVVM0xg0vEdcJeubm2Goyb0M3bst0DjWRnRMOCj0KnfOqXV10gdDjq0yiulFSPO2SQKX5ZOZnOPQCbXOlanw5o5fpv580Sa5u5g7f1v0yRKScQDoQFtpIZJrxANUysEuTcwZUZkQZYJiMzqZZWObdDJzmspg66EvM7moZ5NwWF7HZfCr6kaZXeBOjh0QpSoyBvmOq0Emh85KXNZeZUaLg66d6l6w6666n60000KdyR16081R6K8c03e0WOiyooMCBxS0D7MpMAQTMFK4evm4ZIFZLZP0JE1p600jPPPczs03d9C0yhJJZobdjNaHo2hP9KvBFDkZJiZbTZTuLBOQWSTuYR40jcBjzkdcKZOkk7djSt00O7pBt8hXyHWUWFRdWzZ"
PLACE = "**VV**SVVSS***VV*SSS*VSV*VS*SVSSS*VVVSS*VVS**VVSVV**SVSSSVS**S**VSV*SV*SV**V*VV*"


def plan():
    if not PLAN:
        ops = build()
        link(ops)
        both = [op for op in ops if len(op["q"]) > 1]
        if len(SHIFT) == len(ops) and len(PLACE) == len(both):
            for op, p in zip(both, PLACE):
                op["q"] = op["q"] if p == "*" else p
            seq, total = schedule(ops, 0.0, [(ABC.index(x) - 31) * 0.12 for x in SHIFT])
        else:
            seq, total = schedule(ops, 8.0)
        PLAN["ops"], PLAN["seq"], PLAN["total"] = ops, seq, total
    return PLAN["ops"], PLAN["seq"]


def bits(topo, src, dst):
    return sum(1 << e for e in topo.engines(src, dst)[:NE])


def helper(topo, core, dst):
    for c in topo.cores_of(core):
        if c != core and topo.die(c) == topo.die(core) and topo.may_write(c, dst):
            return c
    return None


def send(g, T, topo, core, dst, out, src, rsem):
    rid, pid = topo.addr(dst, core)
    (ob, o0, o1), (ib, i0, i1) = at(out), at(src)
    g.remote_dma(out_ap=T[ob][:, o0:o1], in_ap=T[ib][:, i0:i1], remote_sem=T.sem[rsem], local_sem=T.sem["lsem"], pid=pid, routing_id=rid, dma_engine_mask=bits(topo, core, dst))


def rank_program(g, core, T, topo):
    rank = T.rank_of(core)
    if rank is None:
        for r, c in enumerate(T.cores):
            dst = T.cores[(r + HOPS[1]) % N]
            if not topo.may_write(c, dst) and helper(topo, c, dst) == core:
                for t in range(1, RO):
                    g.wait_ge(T.sem["h%d" % t], NE)
                    send(g, T, topo, core, dst, "land%d1" % t, "rel%d" % t, "a%d1" % t)
                g.wait_ge(T.sem["lsem"], NE * (RO - 1))
        return
    ops, seq = plan()
    eng = {"V": g.vector, "S": g.scalar, "T": g.tensor, "G": g, "Y": g.sync}
    semn = {"V": "sV", "S": "sS", "T": "sT", "G": "sG"}
    g.sync.dma_start(T.xs[:, :], T.field[:, :]).then_inc(T.sem["dx"], 16)
    g.scalar.dma_start(T.l0[:, :], T.tube[:, :]).then_inc(T.sem["dt"], 16)
    g.scalar.dma_start(T.wi[:, :], T.wt[:, :]).then_inc(T.sem["dw"], 16)
    g.scalar.dma_start(T.ki[:, :], T.kn[:, :]).then_inc(T.sem["dk"], 16)
    g.scalar.dma_start(T.li[:, :], T.lim[:, :]).then_inc(T.sem["dl"], 16)
    count = {q: 0 for q in "VSTG"}
    known = {q: {} for q in "VSTGY"}
    done, snap = {}, {}
    sends = 0
    outs = []
    for k in seq:
        op = ops[k]
        q = op["on"]
        if q == "E":
            done[k] = op["fn"]
            snap[k] = {}
            continue
        e = eng[q]
        need = {}
        for d in sorted(op["deps"]):
            if d in done:
                s, v = done[d]
                if known[q].get(s, 0) < v and need.get(s, (0, 0))[0] < v:
                    need[s] = (v, d)
        for s in sorted(need):
            v, d = need[s]
            if any(snap[d2].get(s, 0) >= v for s2, (v2, d2) in need.items() if s2 != s):
                continue
            e.wait_ge(T.sem[s], v)
        for s, (v, d) in need.items():
            kn_ = known[q]
            kn_[s] = max(kn_.get(s, 0), v)
            for s2, v2 in snap[d].items():
                kn_[s2] = max(kn_.get(s2, 0), v2)
        snap[k] = dict(known[q])
        if op.get("send"):
            t, b, nb = op["send"]
            dst = T.cores[(rank + HOPS[b]) % N]
            if topo.may_write(core, dst):
                send(g, T, topo, core, dst, "land%d%d" % (t + 1, b), nb, "a%d%d" % (t + 1, b))
            else:
                send(g, T, topo, core, helper(topo, core, dst), "rel%d" % (t + 1), nb, "h%d" % (t + 1))
            sends += 1
        elif q == "Y":
            o, h0, h1, src, sm = op["fn"]
            e.dma_start(T[o][:, h0:h1], T[src][:, :]).then_inc(T.sem[sm], 16)
            outs.append(sm)
        else:
            ins = op["fn"](e, T, q == "S") if op.get("gat") else op["fn"](e, T)
            for x in ins:
                x.then_inc(T.sem[semn[q]], 1)
            count[q] += len(ins)
            done[k] = (semn[q], count[q])
    for sm in outs:
        g.sync.wait_ge(T.sem[sm], 16)
    for q in "VSTG":
        if count[q]:
            g.sync.wait_ge(T.sem[semn[q]], count[q])
    g.wait_ge(T.sem["lsem"], NE * sends)
